import numpy as np
import ml_dtypes


def mxq(x, axis, fmt="e4m3"):
    dtype, down = {"e4m3": (ml_dtypes.float8_e4m3fn, 7), "e5m2": (ml_dtypes.float8_e5m2, 14)}[fmt]
    v = np.moveaxis(np.asarray(x, np.float32).astype(ml_dtypes.bfloat16).astype(np.float64), axis, -1)
    blocks = v.reshape(v.shape[:-1] + (-1, 32))
    amax = np.abs(blocks).max(-1, keepdims=True)
    byte = np.maximum(np.where(amax > 0, np.frexp(amax)[1] - 1 + 127, 0) - down, 1)
    scale = np.exp2(byte - 127.0)
    codes = (blocks / scale).astype(np.float32).astype(dtype).astype(np.float64)
    return np.moveaxis((codes * scale).reshape(v.shape), -1, axis)


WIDE = False


def mx_kscale(k):
    if not WIDE:
        return np.ones(k)
    levels = np.array([10, -10, 5, -5, 0])
    if k % 512:
        return np.exp2(np.random.permutation(np.resize(levels, k // 32))).repeat(32)
    a = np.empty((k // 512, 16))
    for p in range(k // 512):
        a[p, :8] = np.random.permutation(np.resize(levels, 8))
        for g in range(8):
            far = levels[np.abs(levels - a[p, g]) >= 10]
            a[p, g + 8] = far[np.random.randint(len(far))]
    return np.exp2(a.ravel()).repeat(32)


def f64(x):
    return np.asarray(x).astype(np.float64)


def striped(idx):
    return np.tile(np.asarray(idx).reshape(-1, 16).T, (8, 1)).astype(np.uint16)


def unstriped(offs):
    return offs[:16].T.reshape(-1).astype(np.int64)


E2M1 = np.array([0.0, 0.5, 1.0, 1.5, 2.0, 3.0, 4.0, 6.0, -0.0, -0.5, -1.0, -1.5, -2.0, -3.0, -4.0, -6.0])


def pack_weight(w, fmt):
    k, n = w.shape
    w = f64(np.asarray(w, np.float32).astype(ml_dtypes.bfloat16)).reshape(k // 32, 32, n)
    amax = np.abs(w).max(1)
    if fmt == "e4m3":
        byte = np.frexp(amax)[1] - 1 + 127 - 7
    else:
        mant, ex = np.frexp(amax / 6.0)
        byte = np.where(mant > 0.5, ex, ex - 1) + 127
    byte = np.clip(np.where(amax > 0, byte, 1), 1, 254)
    scaled = (w * np.exp2(127.0 - byte)[:, None, :]).reshape(k, n).astype(np.float32)
    by_word = np.ascontiguousarray(scaled.reshape(k // 512, 128, 4, n).transpose(0, 1, 3, 2))
    if fmt == "e4m3":
        words = by_word.astype(ml_dtypes.float8_e4m3fn).view(np.uint8)
    else:
        c = by_word.astype(ml_dtypes.float4_e2m1fn).view(np.uint8) & 0xF
        words = (c[..., 0::2] | (c[..., 1::2] << 4)).reshape(k // 512, 128, 2 * n)
    return np.ascontiguousarray(words), np.ascontiguousarray(byte.astype(np.uint8).reshape(k // 512, 16, n))


def unpack_weight(words, scales, fmt):
    g, _, n = scales.shape
    words = np.ascontiguousarray(words).reshape(g, 128, n, -1)
    if fmt == "e4m3":
        vals = words.view(ml_dtypes.float8_e4m3fn).astype(np.float64)
    else:
        nib = np.empty((g, 128, n, 4), np.uint8)
        nib[..., 0::2] = words & 0xF
        nib[..., 1::2] = words >> 4
        vals = E2M1[nib]
    vals = vals * np.repeat(np.exp2(scales.astype(np.float64) - 127.0), 8, axis=1)[..., None]
    return vals.transpose(0, 1, 3, 2).reshape(g * 512, n)


B, N, T, D, NQ = 1, 512, 2048, 1024, 512
DV = 512


def sgn(shape):
    return np.random.uniform(0.5, 2.0, shape) * np.where(np.random.standard_normal(shape) < 0, -1.0, 1.0)


def setup_inputs():
    n = np.random.standard_normal
    idx = np.random.permutation(T)[:B * N]
    s = mx_kscale(D)[:, None]
    u = mx_kscale(N)
    ut = np.ones(T)
    ut[idx] = u
    kp = pack_weight(n((D, T)) / s, "e2m1")
    cp = pack_weight(n((D, T)) / s / 12, "e2m1")
    return {
        "qT": (n((B, D, NQ)) * s * (1.00 / np.sqrt(D))).astype(np.float32),
        "k_words": np.ascontiguousarray(kp[0].reshape(1, 2, 128, T, 2).transpose(0, 2, 3, 1, 4)).reshape(1, 128, T, 4),
        "k_scales": kp[1],
        "c_words": np.ascontiguousarray(cp[0].reshape(1, 2, 128, T, 2).transpose(0, 2, 3, 1, 4)).reshape(1, 128, T, 4),
        "c_scales": cp[1],
        "vT": (n((DV, T)) / ut).astype(np.float32),
        "nb": np.tile(0.5 * n(2048), (128, 1)).astype(np.float32),
        "us": (sgn((B, N, 1)) * u[:, None]).astype(np.float32),
        "offs": striped(idx),
    }


def reference(qT, k_words, k_scales, c_words, c_scales, vT, nb, us, offs):
    idx = unstriped(offs)
    pick = lambda x, which: x[:, which].reshape(x.shape[0], B, -1).transpose(1, 0, 2)
    k = unpack_weight(k_words.reshape(1, 128, T, 2, 2).transpose(0, 3, 1, 2, 4).reshape(2, 128, 2 * T), k_scales, "e2m1")
    kg = pick(k, idx)
    c = unpack_weight(c_words.reshape(1, 128, T, 2, 2).transpose(0, 3, 1, 2, 4).reshape(2, 128, 2 * T), c_scales, "e2m1")
    cg = pick(c, idx)
    qq = mxq(f64(qT), 1, "e4m3")
    a = (kg.transpose(0, 2, 1) @ qq) + (cg.transpose(0, 2, 1) @ qq)
    y = np.maximum(a + pick(f64(nb), idx)[:, :1, :].transpose(0, 2, 1), 0.0) * f64(us)
    wq = mxq(y, 1, "e4m3")
    o = wq.transpose(0, 2, 1) @ mxq(pick(f64(vT), idx).transpose(0, 2, 1), 1, "e4m3")
    return o

@@ -1,0 +1,234 @@
+from contextlib import ExitStack
+
+import concourse.mybir as mybir
+from concourse.masks import make_identity
+
+D, T, N, NQ, DV = 1024, 2048, 512, 512, 512
+FLOPS = 2 * (2 * D * N * NQ + N * NQ * DV)
+BYTES = 4 * (D * NQ + 2 * 128 * T + DV * T + T + N + NQ * DV) + 2 * 32 * T + 2 * 128 * (N // 16)
+
+F32 = mybir.dt.float32
+BF16 = mybir.dt.bfloat16
+I32 = mybir.dt.int32
+U32 = mybir.dt.uint32
+U16 = mybir.dt.uint16
+U8 = mybir.dt.uint8
+FP8X4 = mybir.dt.float8_e4m3fn_x4
+FP4X4 = mybir.dt.float4_e2m1fn_x4
+ACT = mybir.ActivationFunctionType
+ALU = mybir.AluOpType
+
+P = 128
+PACK = 4
+PASSES = D // (P * PACK)
+STREAM_BUFS = 3
+
+
+def tile_attend_mlp_resid_topk_kernel(tc, qT, k_words, k_scales, c_words, c_scales, vT, nb, us, offs, out):
+    nc = tc.nc
+    with ExitStack() as ctx:
+        keep = ctx.enter_context(tc.tile_pool(name="keep", bufs=1))
+        psum = ctx.enter_context(tc.psum_pool(name="psum", bufs=1))
+
+        offsets = keep.tile([P, N // 16], U16, name="offsets")
+        streamed = []
+
+        def stream_tile(dtype):
+            n = len(streamed)
+            t = keep.tile([P, T], dtype, name="stream%d" % n, tag="stream%d" % (n % STREAM_BUFS))
+            streamed.append(t)
+            return t
+
+        def load_q(o):
+            raw = stream_tile(F32)
+            nc.sync.dma_start(out=raw[:], in_=qT[0, 512 * o : 512 * (o + 1), :].rearrange("(p j) w -> p (j w)", j=PACK))
+            return raw
+
+        def load_words(words):
+            win = stream_tile(U32)
+            nc.sync.dma_start(out=win[:].bitcast(I32), in_=words[0].rearrange("p t b -> p (t b)").bitcast(I32))
+            return win
+
+        def load_scales(scales, name, queue):
+            win = keep.tile([P, T], U8, name=name)
+            nc.vector.memset(win[:].bitcast(I32), 0)
+            for quad in range(4):
+                queue.dma_start(
+                    out=win[32 * quad : 32 * quad + 4 * PASSES, :].bitcast(I32),
+                    in_=scales[:, 4 * quad : 4 * quad + 4, :].bitcast(I32),
+                )
+            return win
+
+        q_raw = [load_q(0)]
+        nc.sync.dma_start(offsets[:], offs)
+        q_raw.append(load_q(1))
+        k_win = load_words(k_words)
+
+        ident = keep.tile([P, P], F32, name="ident")
+        make_identity(nc, ident[:])
+        ks_win = load_scales(k_scales, "ks_win", nc.gpsimd)
+        cs_win = load_scales(c_scales, "cs_win", nc.gpsimd)
+        nb_win = keep.tile([P, T], F32, name="nb_win")
+        nc.vector.memset(nb_win[:], 0.0)
+        nc.scalar.dma_start(out=nb_win[0:1, :], in_=nb[0:1, :])
+        nb_dealt = keep.tile([P, N], F32, name="nb_dealt")
+        nc.vector.memset(nb_dealt[:], 0.0)
+        nc.scalar.dma_start(
+            out=nb_dealt[32 : 32 + PACK, 0:P].rearrange("t (g j) -> t g j", j=4),
+            in_=us[0].rearrange("(g t j) one -> t g (j one)", t=PACK, j=4),
+        )
+
+        def gather_scales(win, name):
+            got = keep.tile([P, N], U8, name=name + "_got")
+            nc.vector.tensor_copy(got[:], win[:].indirect(offsets[:]))
+            dealt = keep.tile([P, N], U8, name=name + "_dealt", align_bytes=64)
+            nc.vector.tensor_copy(
+                dealt[:].bitcast(I32).rearrange("p (t g) -> p t g", t=PACK),
+                got[:].bitcast(I32).rearrange("p (g t) -> p t g", t=PACK),
+            )
+            lifted = keep.tile([P, N], U8, name=name + "_lifted", align_bytes=64)
+            nc.vector.memset(lifted[:].bitcast(I32), 0)
+            nc.gpsimd.dma_start(out=lifted[0:100, :].bitcast(I32), in_=dealt[4:104, :].bitcast(I32))
+            return [dealt, lifted]
+
+        def gather_words(win, name):
+            got = keep.tile([P, N], U32, name=name + "_got")
+            nc.vector.tensor_copy(got[:], win[:].indirect(offsets[:]))
+            dealt = keep.tile([P, 4 * N], U8, name=name + "_dealt", align_bytes=64)
+            nc.vector.tensor_copy(
+                dealt[:].bitcast(U16).rearrange("p (t o g j) -> p t o g j", t=PACK, o=PASSES, j=4),
+                got[:].bitcast(U16).rearrange("p (g t j o) -> p t o g j", t=PACK, o=PASSES, j=4),
+            )
+            return dealt
+
+        def quantize(src, width, name):
+            codes = keep.tile([P, width], U32, name=name + "_codes", align_bytes=64)
+            scales = keep.tile([P, width], U8, name=name + "_scales", align_bytes=64)
+            nc.vector.quantize_mx(out=codes[:].bitcast(FP8X4), scales=scales[:], in_=src)
+            return codes, scales
+
+        def interleave_q(o):
+            grouped = keep.tile([P, NQ * PACK], BF16, name="q_grouped%d" % o, align_bytes=64)
+            nc.scalar.activation(
+                grouped[:].rearrange("p (c i t) -> p c t i", i=4, t=PACK),
+                q_raw[o][:].rearrange("p (t c i) -> p c t i", i=4, t=PACK),
+                ACT.Copy,
+            )
+            return grouped
+
+        nb_got = keep.tile([P, N], F32, name="nb_got")
+        nc.vector.tensor_copy(nb_got[:], nb_win[:].indirect(offsets[:]))
+        ks = gather_scales(ks_win, "ks")
+        q_grouped = [interleave_q(0)]
+        c_win = load_words(c_words)
+        nc.scalar.copy(
+            nb_dealt[0:32, :].rearrange("p (t g j) -> p t g j", t=PACK, j=4),
+            nb_got[0:32, :].rearrange("p (g t j) -> p t g j", t=PACK, j=4),
+        )
+        nb_ps = psum.tile([P, N], F32, name="nb_ps", tag="turn0")
+        for t in range(PACK):
+            nc.tensor.transpose(nb_ps[:, t * P : (t + 1) * P], nb_dealt[:, t * P : (t + 1) * P], ident[:])
+        nb_col = keep.tile([P, PACK], F32, name="nb_col")
+        nc.scalar.copy(nb_col[:], nb_ps[:, 0:N:P])
+        us_col = keep.tile([P, PACK], F32, name="us_col")
+        nc.scalar.copy(us_col[:], nb_ps[:, 32 : 32 + PACK])
+
+        q_grouped.append(interleave_q(1))
+        q_mx = [quantize(q_grouped[0][:], NQ, "q0")]
+        cs = gather_scales(cs_win, "cs")
+        q_mx.append(quantize(q_grouped[1][:], NQ, "q1"))
+
+        def load_v(b):
+            win = stream_tile(F32)
+            nc.sync.dma_start(out=win[:], in_=vT[b * P : (b + 1) * P, :])
+            return win
+
+        v_win = [load_v(0)]
+        kw = gather_words(k_win, "kw")
+        v_win.append(load_v(1))
+        cw = gather_words(c_win, "cw")
+        v_win.append(load_v(2))
+
+        banks = [psum.tile([P, NQ], F32, name="score%d" % t) for t in range(PACK)]
+
+        def score_pass(t, o, words, scales, start, stop):
+            col = (t * PASSES + o) * P
+            nc.tensor.matmul_mx(
+                out=banks[t][:],
+                lhsT=words[:, 2 * col : 2 * (col + P)].bitcast(FP4X4),
+                lhsT_scale=scales[o][:, t * P : (t + 1) * P],
+                rhs=q_mx[o][0][:].bitcast(FP8X4),
+                rhs_scale=q_mx[o][1][:],
+                start=start,
+                stop=stop,
+            )
+
+        for t in range(PACK):
+            for o in range(PASSES):
+                score_pass(t, o, kw, ks, o == 0, False)
+        hidden = keep.tile([P, PACK * NQ], F32, name="hidden")
+        for t in range(PACK):
+            for o in range(PASSES):
+                score_pass(t, o, cw, cs, False, o == PASSES - 1)
+            nc.scalar.activation(hidden[:, t * NQ : (t + 1) * NQ], banks[t][:], ACT.Relu, bias=nb_col[:, t : t + 1])
+
+        def prepare_v(b):
+            got = keep.tile([P, N], BF16, name="v_got%d" % b)
+            nc.vector.tensor_copy(
+                got[:].rearrange("p (u g j w) -> p g u w j", u=2, j=4, w=2),
+                v_win[b][:].indirect(offsets[:]),
+            )
+            turned = psum.tile([P, 2 * P], F32, name="turned%d" % b, tag="turn%d" % ((b + 1) % 2))
+            words = got[:].bitcast(F32)
+            for u in range(2):
+                nc.tensor.transpose(turned[:, u * P : (u + 1) * P], words[:, u * P : (u + 1) * P], ident[:])
+            grouped = keep.tile([P, P * PACK], BF16, name="v_grouped%d" % b, align_bytes=64)
+            nc.scalar.copy(
+                grouped[:].bitcast(F32).rearrange("p (e u) -> p e u", u=2),
+                turned[:].rearrange("p (u e) -> p e u", u=2),
+            )
+            return quantize(grouped[:], P, "v%d" % b)
+
+        v_mx = [prepare_v(0)]
+        v_win.append(load_v(3))
+        v_mx.append(prepare_v(1))
+
+        y = keep.tile([P, NQ * PACK], BF16, name="y", align_bytes=64)
+        nc.vector.tensor_tensor(
+            y[:].rearrange("p (c i t) -> p c t i", i=4, t=PACK),
+            hidden[:].rearrange("p (t c i) -> p c t i", i=4, t=PACK),
+            us_col[:].unsqueeze(1).unsqueeze(3).to_broadcast([P, NQ // 4, PACK, 4]),
+            ALU.mult,
+        )
+        v_mx.append(prepare_v(2))
+        y_codes, y_scales = quantize(y[:], NQ, "y")
+
+        out_rows = out[0].rearrange("(a p) e -> p a e", p=P)
+
+        def finish(b, halves):
+            result = keep.tile([P, PACK * P], F32, name="result%d" % b)
+            for h, (engine, queue) in enumerate(halves):
+                width = PACK // len(halves)
+                acc = psum.tile([P, width * P], F32, name="acc%d_%d" % (b, h), tag="acc%d" % ((b + h + 1) % 2))
+                for i in range(width):
+                    a = h * width + i
+                    nc.tensor.matmul_mx(
+                        out=acc[:, i * P : (i + 1) * P],
+                        lhsT=y_codes[:, a * P : (a + 1) * P].bitcast(FP8X4),
+                        lhsT_scale=y_scales[:, a * P : (a + 1) * P],
+                        rhs=v_mx[b][0][:].bitcast(FP8X4),
+                        rhs_scale=v_mx[b][1][:],
+                        start=True,
+                        stop=True,
+                    )
+                part = result[:, h * width * P : (h + 1) * width * P]
+                engine(part, acc[:])
+                queue.dma_start(
+                    out=out_rows[:, h * width : (h + 1) * width, b * P : (b + 1) * P],
+                    in_=part.rearrange("p (a e) -> p a e", e=P),
+                )
+
+        for b in range(3):
+            finish(b, [(nc.scalar.copy, nc.sync)])
+        v_mx.append(prepare_v(3))
+        finish(3, [(nc.scalar.copy, nc.scalar), (nc.vector.tensor_copy, nc.sync)])

@@ -21,7 +21,6 @@ ALU = mybir.AluOpType
 P = 128
 PACK = 4
 PASSES = D // (P * PACK)
-STREAM_BUFS = 3
 
 
 def tile_attend_mlp_resid_topk_kernel(tc, qT, k_words, k_scales, c_words, c_scales, vT, nb, us, offs, out):
@@ -31,52 +30,45 @@ def tile_attend_mlp_resid_topk_kernel(tc, qT, k_words, k_scales, c_words, c_scal
         psum = ctx.enter_context(tc.psum_pool(name="psum", bufs=1))
 
         offsets = keep.tile([P, N // 16], U16, name="offsets")
-        streamed = []
-
-        def stream_tile(dtype):
-            n = len(streamed)
-            t = keep.tile([P, T], dtype, name="stream%d" % n, tag="stream%d" % (n % STREAM_BUFS))
-            streamed.append(t)
-            return t
+        def stream_tile(dtype, name, buffer):
+            return keep.tile([P, T], dtype, name=name, tag="stream" + buffer)
 
         def load_q(o):
-            raw = stream_tile(F32)
+            raw = stream_tile(F32, "q_raw%d" % o, "AB"[o])
             nc.sync.dma_start(out=raw[:], in_=qT[0, 512 * o : 512 * (o + 1), :].rearrange("(p j) w -> p (j w)", j=PACK))
             return raw
 
-        def load_words(words):
-            win = stream_tile(U32)
+        def load_words(words, name, buffer):
+            win = stream_tile(U32, name, buffer)
             nc.sync.dma_start(out=win[:].bitcast(I32), in_=words[0].rearrange("p t b -> p (t b)").bitcast(I32))
             return win
 
-        def load_scales(scales, name, queue):
+        def load_scales(scales, name, queues):
             win = keep.tile([P, T], U8, name=name)
             nc.vector.memset(win[:].bitcast(I32), 0)
-            for quad in range(4):
-                queue.dma_start(
-                    out=win[32 * quad : 32 * quad + 4 * PASSES, :].bitcast(I32),
-                    in_=scales[:, 4 * quad : 4 * quad + 4, :].bitcast(I32),
-                )
+            rows = scales.bitcast(I32).rearrange("o (quad i) t -> i quad o t", i=4)
+            for i in range(4):
+                queues[i].dma_start(out=win[i:P:16, :].bitcast(I32), in_=rows[i])
             return win
 
         q_raw = [load_q(0)]
         nc.sync.dma_start(offsets[:], offs)
         q_raw.append(load_q(1))
-        k_win = load_words(k_words)
 
-        ident = keep.tile([P, P], F32, name="ident")
-        make_identity(nc, ident[:])
-        ks_win = load_scales(k_scales, "ks_win", nc.gpsimd)
-        cs_win = load_scales(c_scales, "cs_win", nc.gpsimd)
-        nb_win = keep.tile([P, T], F32, name="nb_win")
+        cs_win = load_scales(c_scales, "cs_win", [nc.gpsimd] * 4)
+        nb_win = stream_tile(F32, "nb_win", "C")
         nc.vector.memset(nb_win[:], 0.0)
         nc.scalar.dma_start(out=nb_win[0:1, :], in_=nb[0:1, :])
-        nb_dealt = keep.tile([P, N], F32, name="nb_dealt")
-        nc.vector.memset(nb_dealt[:], 0.0)
+        ks_win = load_scales(k_scales, "ks_win", [nc.scalar] * 4)
+        us_rows = keep.tile([P, P], F32, name="us_rows")
+        nc.vector.memset(us_rows[:], 0.0)
         nc.scalar.dma_start(
-            out=nb_dealt[32 : 32 + PACK, 0:P].rearrange("t (g j) -> t g j", j=4),
+            out=us_rows[32 : 32 + PACK, :].rearrange("t (g j) -> t g j", j=4),
             in_=us[0].rearrange("(g t j) one -> t g (j one)", t=PACK, j=4),
         )
+        ident = keep.tile([P, P], F32, name="ident")
+        nc.vector.memset(ident[:], 0.0)
+        make_identity(nc, ident[:], nomemset=True)
 
         def gather_scales(win, name):
             got = keep.tile([P, N], U8, name=name + "_got")
@@ -88,7 +80,7 @@ def tile_attend_mlp_resid_topk_kernel(tc, qT, k_words, k_scales, c_words, c_scal
             )
             lifted = keep.tile([P, N], U8, name=name + "_lifted", align_bytes=64)
             nc.vector.memset(lifted[:].bitcast(I32), 0)
-            nc.gpsimd.dma_start(out=lifted[0:100, :].bitcast(I32), in_=dealt[4:104, :].bitcast(I32))
+            nc.sync.dma_start(out=lifted[0:100, :].bitcast(I32), in_=dealt[16:116, :].bitcast(I32))
             return [dealt, lifted]
 
         def gather_words(win, name):
@@ -108,7 +100,7 @@ def tile_attend_mlp_resid_topk_kernel(tc, qT, k_words, k_scales, c_words, c_scal
             return codes, scales
 
         def interleave_q(o):
-            grouped = keep.tile([P, NQ * PACK], BF16, name="q_grouped%d" % o, align_bytes=64)
+            grouped = keep.tile([P, NQ * PACK], BF16, name="q_grouped%d" % o, tag="q_grouped%d" % o, align_bytes=64)
             nc.scalar.activation(
                 grouped[:].rearrange("p (c i t) -> p c t i", i=4, t=PACK),
                 q_raw[o][:].rearrange("p (t c i) -> p c t i", i=4, t=PACK),
@@ -118,28 +110,33 @@ def tile_attend_mlp_resid_topk_kernel(tc, qT, k_words, k_scales, c_words, c_scal
 
         nb_got = keep.tile([P, N], F32, name="nb_got")
         nc.vector.tensor_copy(nb_got[:], nb_win[:].indirect(offsets[:]))
+        k_win = load_words(k_words, "k_win", "C")
         ks = gather_scales(ks_win, "ks")
         q_grouped = [interleave_q(0)]
-        c_win = load_words(c_words)
-        nc.scalar.copy(
-            nb_dealt[0:32, :].rearrange("p (t g j) -> p t g j", t=PACK, j=4),
-            nb_got[0:32, :].rearrange("p (g t j) -> p t g j", t=PACK, j=4),
-        )
-        nb_ps = psum.tile([P, N], F32, name="nb_ps", tag="turn0")
-        for t in range(PACK):
-            nc.tensor.transpose(nb_ps[:, t * P : (t + 1) * P], nb_dealt[:, t * P : (t + 1) * P], ident[:])
-        nb_col = keep.tile([P, PACK], F32, name="nb_col")
-        nc.scalar.copy(nb_col[:], nb_ps[:, 0:N:P])
-        us_col = keep.tile([P, PACK], F32, name="us_col")
-        nc.scalar.copy(us_col[:], nb_ps[:, 32 : 32 + PACK])
+        c_win = load_words(c_words, "c_win", "A")
 
         q_grouped.append(interleave_q(1))
         q_mx = [quantize(q_grouped[0][:], NQ, "q0")]
         cs = gather_scales(cs_win, "cs")
         q_mx.append(quantize(q_grouped[1][:], NQ, "q1"))
 
+        nb_dealt = keep.tile([P, N], F32, name="nb_dealt", tag="q_grouped0", align_bytes=64)
+        nc.scalar.copy(
+            nb_dealt[:].rearrange("p (t g j) -> p t g j", t=PACK, j=4),
+            nb_got[:].rearrange("p (g t j) -> p t g j", t=PACK, j=4),
+        )
+        nb_ps = psum.tile([P, N], F32, name="nb_ps", tag="turn0")
+        nc.tensor.matmul(nb_ps[:, 0:P], us_rows[:], ident[:], start=True, stop=False, is_transpose=True)
+        nc.tensor.matmul(nb_ps[:, 0:P], nb_dealt[:, 0:P], ident[:], start=False, stop=True, is_transpose=True)
+        for t in range(1, PACK):
+            nc.tensor.transpose(nb_ps[:, t * P : (t + 1) * P], nb_dealt[:, t * P : (t + 1) * P], ident[:])
+        nb_col = keep.tile([P, PACK], F32, name="nb_col")
+        nc.scalar.copy(nb_col[:], nb_ps[:, 0:N:P])
+        us_col = keep.tile([P, PACK], F32, name="us_col")
+        nc.scalar.copy(us_col[:], nb_ps[:, 32 : 32 + PACK])
+
         def load_v(b):
-            win = stream_tile(F32)
+            win = stream_tile(F32, "v_win%d" % b, "BCAB"[b])
             nc.sync.dma_start(out=win[:], in_=vT[b * P : (b + 1) * P, :])
             return win
 

@@ -1,7 +1,6 @@
 from contextlib import ExitStack
 
 import concourse.mybir as mybir
-from concourse.masks import make_identity
 
 D, T, N, NQ, DV = 1024, 2048, 512, 512, 512
 FLOPS = 2 * (2 * D * N * NQ + N * NQ * DV)
@@ -27,11 +26,14 @@ def tile_attend_mlp_resid_topk_kernel(tc, qT, k_words, k_scales, c_words, c_scal
     nc = tc.nc
     with ExitStack() as ctx:
         keep = ctx.enter_context(tc.tile_pool(name="keep", bufs=1))
+        shared = ctx.enter_context(tc.tile_pool(name="shared", bufs=1))
+        stream = ctx.enter_context(tc.tile_pool(name="stream", bufs=1))
         psum = ctx.enter_context(tc.psum_pool(name="psum", bufs=1))
 
         offsets = keep.tile([P, N // 16], U16, name="offsets")
+
         def stream_tile(dtype, name, buffer):
-            return keep.tile([P, T], dtype, name=name, tag="stream" + buffer)
+            return stream.tile([P, T], dtype, name=name, offset=4 * T * "ABC".index(buffer), align_bytes=64)
 
         def load_q(o):
             raw = stream_tile(F32, "q_raw%d" % o, "AB"[o])
@@ -43,48 +45,49 @@ def tile_attend_mlp_resid_topk_kernel(tc, qT, k_words, k_scales, c_words, c_scal
             nc.sync.dma_start(out=win[:].bitcast(I32), in_=words[0].rearrange("p t b -> p (t b)").bitcast(I32))
             return win
 
-        def load_scales(scales, name, queues):
-            win = keep.tile([P, T], U8, name=name)
+        def load_scales(scales, win):
             nc.vector.memset(win[:].bitcast(I32), 0)
-            rows = scales.bitcast(I32).rearrange("o (quad i) t -> i quad o t", i=4)
-            for i in range(4):
-                queues[i].dma_start(out=win[i:P:16, :].bitcast(I32), in_=rows[i])
-            return win
+            nc.scalar.dma_start(out=win[0:P:4, :].bitcast(I32), in_=scales.bitcast(I32).rearrange("o f t -> f o t"))
 
-        q_raw = [load_q(0)]
         nc.sync.dma_start(offsets[:], offs)
+        q_raw = [load_q(0)]
         q_raw.append(load_q(1))
+        k_win = load_words(k_words, "k_win", "C")
 
-        cs_win = load_scales(c_scales, "cs_win", [nc.gpsimd] * 4)
-        nb_win = stream_tile(F32, "nb_win", "C")
+        distance = keep.tile([P, P], F32, name="distance")
+        nc.gpsimd.iota(distance[:], [[1, P]], base=0, channel_multiplier=-1, allow_small_or_imprecise_dtypes=True)
+        magnitude = keep.tile([P, P], F32, name="magnitude")
+        nc.scalar.activation(magnitude[:], distance[:], ACT.Abs)
+        ident = keep.tile([P, P], F32, name="ident")
+        nc.scalar.activation(ident[:], magnitude[:], ACT.Relu, bias=1.0, scale=-1.0)
+
+        ks_win = keep.tile([P, T], U8, name="ks_win")
+        load_scales(k_scales, ks_win)
+        cs_win = keep.tile([P, T], U8, name="cs_win")
+        load_scales(c_scales, cs_win)
+        nb_win = keep.tile([P, T], F32, name="nb_win")
         nc.vector.memset(nb_win[:], 0.0)
-        nc.scalar.dma_start(out=nb_win[0:1, :], in_=nb[0:1, :])
-        ks_win = load_scales(k_scales, "ks_win", [nc.scalar] * 4)
+        nc.gpsimd.dma_start(out=nb_win[0:1, :], in_=nb[0:1, :])
         us_rows = keep.tile([P, P], F32, name="us_rows")
         nc.vector.memset(us_rows[:], 0.0)
-        nc.scalar.dma_start(
+        nc.gpsimd.dma_start(
             out=us_rows[32 : 32 + PACK, :].rearrange("t (g j) -> t g j", j=4),
             in_=us[0].rearrange("(g t j) one -> t g (j one)", t=PACK, j=4),
         )
-        ident = keep.tile([P, P], F32, name="ident")
-        nc.vector.memset(ident[:], 0.0)
-        make_identity(nc, ident[:], nomemset=True)
 
-        def gather_scales(win, name):
-            got = keep.tile([P, N], U8, name=name + "_got")
+        scales_dealt = keep.tile([P, 2 * N], U8, name="scales_dealt")
+        planes = keep.tile([P, PASSES * 2 * N], U8, name="planes", align_bytes=64)
+        nc.vector.memset(planes[:].bitcast(I32), 0)
+
+        def gather_scales(win, table):
+            got = keep.tile([P, N], U8, name="scales_got%d" % table)
             nc.vector.tensor_copy(got[:], win[:].indirect(offsets[:]))
-            dealt = keep.tile([P, N], U8, name=name + "_dealt", align_bytes=64)
             nc.vector.tensor_copy(
-                dealt[:].bitcast(I32).rearrange("p (t g) -> p t g", t=PACK),
+                scales_dealt[:, table * N : (table + 1) * N].bitcast(I32).rearrange("p (t g) -> p t g", t=PACK),
                 got[:].bitcast(I32).rearrange("p (g t) -> p t g", t=PACK),
             )
-            lifted = keep.tile([P, N], U8, name=name + "_lifted", align_bytes=64)
-            nc.vector.memset(lifted[:].bitcast(I32), 0)
-            nc.sync.dma_start(out=lifted[0:100, :].bitcast(I32), in_=dealt[16:116, :].bitcast(I32))
-            return [dealt, lifted]
 
-        def gather_words(win, name):
-            got = keep.tile([P, N], U32, name=name + "_got")
+        def gather_words(win, got, name):
             nc.vector.tensor_copy(got[:], win[:].indirect(offsets[:]))
             dealt = keep.tile([P, 4 * N], U8, name=name + "_dealt", align_bytes=64)
             nc.vector.tensor_copy(
@@ -93,34 +96,36 @@ def tile_attend_mlp_resid_topk_kernel(tc, qT, k_words, k_scales, c_words, c_scal
             )
             return dealt
 
-        def quantize(src, width, name):
-            codes = keep.tile([P, width], U32, name=name + "_codes", align_bytes=64)
+        def quantize(src, width, name, pool=keep, offset=None):
+            codes = pool.tile([P, width], U32, name=name + "_codes", offset=offset, align_bytes=64)
             scales = keep.tile([P, width], U8, name=name + "_scales", align_bytes=64)
             nc.vector.quantize_mx(out=codes[:].bitcast(FP8X4), scales=scales[:], in_=src)
             return codes, scales
 
-        def interleave_q(o):
-            grouped = keep.tile([P, NQ * PACK], BF16, name="q_grouped%d" % o, tag="q_grouped%d" % o, align_bytes=64)
-            nc.scalar.activation(
+        def interleave_q(o, grouped):
+            nc.scalar.copy(
                 grouped[:].rearrange("p (c i t) -> p c t i", i=4, t=PACK),
                 q_raw[o][:].rearrange("p (t c i) -> p c t i", i=4, t=PACK),
-                ACT.Copy,
             )
-            return grouped
 
-        nb_got = keep.tile([P, N], F32, name="nb_got")
-        nc.vector.tensor_copy(nb_got[:], nb_win[:].indirect(offsets[:]))
-        k_win = load_words(k_words, "k_win", "C")
-        ks = gather_scales(ks_win, "ks")
-        q_grouped = [interleave_q(0)]
+        gather_scales(ks_win, 0)
+        gather_scales(cs_win, 1)
+        for quad in range(4):
+            nc.sync.dma_start(
+                out=planes[32 * quad : 32 * quad + 4, :].bitcast(I32).rearrange("i (o w) -> i o w", o=PASSES),
+                in_=scales_dealt[32 * quad : 32 * (quad + 1) : 4, :].bitcast(I32),
+            )
+        q_grouped = [shared.tile([P, NQ * PACK], BF16, name="q_grouped0", offset=4 * T, align_bytes=64)]
+        interleave_q(0, q_grouped[0])
         c_win = load_words(c_words, "c_win", "A")
 
-        q_grouped.append(interleave_q(1))
+        q_grouped.append(shared.tile([P, NQ * PACK], BF16, name="q_grouped1", offset=0, align_bytes=64))
+        interleave_q(1, q_grouped[1])
         q_mx = [quantize(q_grouped[0][:], NQ, "q0")]
-        cs = gather_scales(cs_win, "cs")
-        q_mx.append(quantize(q_grouped[1][:], NQ, "q1"))
+        nb_got = shared.tile([P, N], F32, name="nb_got", offset=4 * T + 4 * N, align_bytes=64)
+        nc.vector.tensor_copy(nb_got[:], nb_win[:].indirect(offsets[:]))
 
-        nb_dealt = keep.tile([P, N], F32, name="nb_dealt", tag="q_grouped0", align_bytes=64)
+        nb_dealt = stream.tile([P, N], F32, name="nb_dealt", offset=4 * T, align_bytes=64)
         nc.scalar.copy(
             nb_dealt[:].rearrange("p (t g j) -> p t g j", t=PACK, j=4),
             nb_got[:].rearrange("p (g t j) -> p t g j", t=PACK, j=4),
@@ -136,46 +141,51 @@ def tile_attend_mlp_resid_topk_kernel(tc, qT, k_words, k_scales, c_words, c_scal
         nc.scalar.copy(us_col[:], nb_ps[:, 32 : 32 + PACK])
 
         def load_v(b):
-            win = stream_tile(F32, "v_win%d" % b, "BCAB"[b])
+            win = stream_tile(F32, "v_win%d" % b, "CBA"[b]) if b < 3 else shared.tile([P, T], F32, name="v_win3", offset=0, align_bytes=64)
             nc.sync.dma_start(out=win[:], in_=vT[b * P : (b + 1) * P, :])
             return win
 
-        v_win = [load_v(0)]
-        kw = gather_words(k_win, "kw")
-        v_win.append(load_v(1))
-        cw = gather_words(c_win, "cw")
+        kw = gather_words(k_win, shared.tile([P, N], U32, name="kw_got", offset=4 * T, align_bytes=64), "kw")
+        q_mx.append(quantize(q_grouped[1][:], NQ, "q1", shared, 4 * T))
+        v_win = [load_v(0), load_v(1)]
+        cw = gather_words(c_win, shared.tile([P, N], U32, name="cw_got", offset=0, align_bytes=64), "cw")
         v_win.append(load_v(2))
+        v_win.append(load_v(3))
 
-        banks = [psum.tile([P, NQ], F32, name="score%d" % t) for t in range(PACK)]
+        banks = [psum.tile([P, NQ], F32, name="score%d" % t, tag="score%d" % t) for t in range(PACK)]
 
-        def score_pass(t, o, words, scales, start, stop):
+        def score_pass(t, o, words, table, start, stop):
             col = (t * PASSES + o) * P
+            byte = (2 * o + table) * N + t * P
             nc.tensor.matmul_mx(
                 out=banks[t][:],
                 lhsT=words[:, 2 * col : 2 * (col + P)].bitcast(FP4X4),
-                lhsT_scale=scales[o][:, t * P : (t + 1) * P],
+                lhsT_scale=planes[:, byte : byte + P],
                 rhs=q_mx[o][0][:].bitcast(FP8X4),
                 rhs_scale=q_mx[o][1][:],
                 start=start,
                 stop=stop,
             )
 
+        for o in range(PASSES):
+            for t in range(PACK):
+                score_pass(t, o, kw, 0, o == 0, False)
+        hidden = keep.tile([P, PACK * NQ], F32, name="hidden", tag="hidden", align_bytes=64)
         for t in range(PACK):
             for o in range(PASSES):
-                score_pass(t, o, kw, ks, o == 0, False)
-        hidden = keep.tile([P, PACK * NQ], F32, name="hidden")
-        for t in range(PACK):
-            for o in range(PASSES):
-                score_pass(t, o, cw, cs, False, o == PASSES - 1)
+                score_pass(t, o, cw, 1, False, o == PASSES - 1)
             nc.scalar.activation(hidden[:, t * NQ : (t + 1) * NQ], banks[t][:], ACT.Relu, bias=nb_col[:, t : t + 1])
 
         def prepare_v(b):
-            got = keep.tile([P, N], BF16, name="v_got%d" % b)
+            if b < 2:
+                got = keep.tile([P, N], BF16, name="v_got%d" % b, align_bytes=64)
+            else:
+                got = stream.tile([P, N], BF16, name="v_got%d" % b, offset=4 * T + 2 * N * (b - 2), align_bytes=64)
             nc.vector.tensor_copy(
                 got[:].rearrange("p (u g j w) -> p g u w j", u=2, j=4, w=2),
                 v_win[b][:].indirect(offsets[:]),
             )
-            turned = psum.tile([P, 2 * P], F32, name="turned%d" % b, tag="turn%d" % ((b + 1) % 2))
+            turned = psum.tile([P, 2 * P], F32, name="turned%d" % b, tag="score%d" % (1, 3, 0, 2)[b])
             words = got[:].bitcast(F32)
             for u in range(2):
                 nc.tensor.transpose(turned[:, u * P : (u + 1) * P], words[:, u * P : (u + 1) * P], ident[:])
@@ -184,21 +194,20 @@ def tile_attend_mlp_resid_topk_kernel(tc, qT, k_words, k_scales, c_words, c_scal
                 grouped[:].bitcast(F32).rearrange("p (e u) -> p e u", u=2),
                 turned[:].rearrange("p (u e) -> p e u", u=2),
             )
-            return quantize(grouped[:], P, "v%d" % b)
+            return grouped
 
-        v_mx = [prepare_v(0)]
-        v_win.append(load_v(3))
-        v_mx.append(prepare_v(1))
+        v_grouped = [prepare_v(0), prepare_v(1)]
 
-        y = keep.tile([P, NQ * PACK], BF16, name="y", align_bytes=64)
+        y = stream.tile([P, NQ * PACK], BF16, name="y", offset=4 * T, align_bytes=64)
         nc.vector.tensor_tensor(
             y[:].rearrange("p (c i t) -> p c t i", i=4, t=PACK),
             hidden[:].rearrange("p (t c i) -> p c t i", i=4, t=PACK),
             us_col[:].unsqueeze(1).unsqueeze(3).to_broadcast([P, NQ // 4, PACK, 4]),
             ALU.mult,
         )
-        v_mx.append(prepare_v(2))
         y_codes, y_scales = quantize(y[:], NQ, "y")
+        v_mx = [quantize(v_grouped[b][:], P, "v%d" % b, stream, 4 * T + 4 * N + 4 * P * b) for b in range(2)]
+        v_mx.append(quantize(prepare_v(2)[:], P, "v2"))
 
         out_rows = out[0].rearrange("(a p) e -> p a e", p=P)
 
@@ -227,5 +236,5 @@ def tile_attend_mlp_resid_topk_kernel(tc, qT, k_words, k_scales, c_words, c_scal
 
         for b in range(3):
             finish(b, [(nc.scalar.copy, nc.sync)])
-        v_mx.append(prepare_v(3))
+        v_mx.append(quantize(prepare_v(3)[:], P, "v3"))
         finish(3, [(nc.scalar.copy, nc.scalar), (nc.vector.tensor_copy, nc.sync)])

@@ -1,6 +1,7 @@
 from contextlib import ExitStack
 
 import concourse.mybir as mybir
+from concourse.masks import make_identity
 
 D, T, N, NQ, DV = 1024, 2048, 512, 512, 512
 FLOPS = 2 * (2 * D * N * NQ + N * NQ * DV)
@@ -20,6 +21,8 @@ ALU = mybir.AluOpType
 P = 128
 PACK = 4
 PASSES = D // (P * PACK)
+WINDOW = 4 * T
+STREAM_OFFSETS = {"A": WINDOW // 2, "A0": 0, "A1": WINDOW, "B": 2 * WINDOW, "y": 2 * WINDOW + WINDOW // 2, "gap": 3 * WINDOW, "C": 3 * WINDOW + 2 * N}
 
 
 def tile_attend_mlp_resid_topk_kernel(tc, qT, k_words, k_scales, c_words, c_scales, vT, nb, us, offs, out):
@@ -33,7 +36,7 @@ def tile_attend_mlp_resid_topk_kernel(tc, qT, k_words, k_scales, c_words, c_scal
         offsets = keep.tile([P, N // 16], U16, name="offsets")
 
         def stream_tile(dtype, name, buffer):
-            return stream.tile([P, T], dtype, name=name, offset=4 * T * "ABC".index(buffer), align_bytes=64)
+            return stream.tile([P, T], dtype, name=name, offset=STREAM_OFFSETS[buffer], align_bytes=64)
 
         def load_q(o):
             raw = stream_tile(F32, "q_raw%d" % o, "AB"[o])
@@ -45,21 +48,17 @@ def tile_attend_mlp_resid_topk_kernel(tc, qT, k_words, k_scales, c_words, c_scal
             nc.sync.dma_start(out=win[:].bitcast(I32), in_=words[0].rearrange("p t b -> p (t b)").bitcast(I32))
             return win
 
+        def load_v(b):
+            win = stream_tile(F32, "v_win%d" % b, ("A1", "B", "C", "A0")[b])
+            nc.sync.dma_start(out=win[:], in_=vT[b * P : (b + 1) * P, :])
+            return win
+
         def load_scales(scales, win):
             nc.vector.memset(win[:].bitcast(I32), 0)
-            nc.scalar.dma_start(out=win[0:P:4, :].bitcast(I32), in_=scales.bitcast(I32).rearrange("o f t -> f o t"))
+            nc.sync.dma_start(out=win[0:P:4, :].bitcast(I32), in_=scales.bitcast(I32).rearrange("o f t -> f o t"))
 
         nc.sync.dma_start(offsets[:], offs)
         q_raw = [load_q(0)]
-        q_raw.append(load_q(1))
-        k_win = load_words(k_words, "k_win", "C")
-
-        distance = keep.tile([P, P], F32, name="distance")
-        nc.gpsimd.iota(distance[:], [[1, P]], base=0, channel_multiplier=-1, allow_small_or_imprecise_dtypes=True)
-        magnitude = keep.tile([P, P], F32, name="magnitude")
-        nc.scalar.activation(magnitude[:], distance[:], ACT.Abs)
-        ident = keep.tile([P, P], F32, name="ident")
-        nc.scalar.activation(ident[:], magnitude[:], ACT.Relu, bias=1.0, scale=-1.0)
 
         ks_win = keep.tile([P, T], U8, name="ks_win")
         load_scales(k_scales, ks_win)
@@ -67,15 +66,22 @@ def tile_attend_mlp_resid_topk_kernel(tc, qT, k_words, k_scales, c_words, c_scal
         load_scales(c_scales, cs_win)
         nb_win = keep.tile([P, T], F32, name="nb_win")
         nc.vector.memset(nb_win[:], 0.0)
-        nc.gpsimd.dma_start(out=nb_win[0:1, :], in_=nb[0:1, :])
+        nc.sync.dma_start(out=nb_win[0:1, :], in_=nb[0:1, :])
+
+        zeros = stream.tile([P, 3 * P], F32, name="zeros", offset=STREAM_OFFSETS["gap"] - 2 * P, align_bytes=64)
+        nc.vector.memset(zeros[:, 0:P], 0.0)
         us_rows = keep.tile([P, P], F32, name="us_rows")
-        nc.vector.memset(us_rows[:], 0.0)
-        nc.gpsimd.dma_start(
+        nc.scalar.activation(us_rows[:], zeros[:, 0:P], ACT.Relu)
+        q_raw.append(load_q(1))
+        k_win = load_words(k_words, "k_win", "C")
+        nc.scalar.dma_start(
             out=us_rows[32 : 32 + PACK, :].rearrange("t (g j) -> t g j", j=4),
             in_=us[0].rearrange("(g t j) one -> t g (j one)", t=PACK, j=4),
         )
+        ident = keep.tile([P, P], F32, name="ident")
+        make_identity(nc, ident[:])
 
-        scales_dealt = keep.tile([P, 2 * N], U8, name="scales_dealt")
+        scales_dealt = stream.tile([P, 2 * N], U8, name="scales_dealt", offset=STREAM_OFFSETS["gap"], align_bytes=64)
         planes = keep.tile([P, PASSES * 2 * N], U8, name="planes", align_bytes=64)
         nc.vector.memset(planes[:].bitcast(I32), 0)
 
@@ -90,10 +96,11 @@ def tile_attend_mlp_resid_topk_kernel(tc, qT, k_words, k_scales, c_words, c_scal
         def gather_words(win, got, name):
             nc.vector.tensor_copy(got[:], win[:].indirect(offsets[:]))
             dealt = keep.tile([P, 4 * N], U8, name=name + "_dealt", align_bytes=64)
-            nc.vector.tensor_copy(
-                dealt[:].bitcast(U16).rearrange("p (t o g j) -> p t o g j", t=PACK, o=PASSES, j=4),
-                got[:].bitcast(U16).rearrange("p (g t j o) -> p t o g j", t=PACK, o=PASSES, j=4),
-            )
+            for o in range(PASSES):
+                nc.vector.tensor_copy(
+                    dealt[:].bitcast(U16)[:, o * N : (o + 1) * N].rearrange("p (t g j) -> p t g j", t=PACK, j=4),
+                    got[:].bitcast(U16)[:, o : 2 * N : 2].rearrange("p (g t j) -> p t g j", t=PACK, j=4),
+                )
             return dealt
 
         def quantize(src, width, name, pool=keep, offset=None):
@@ -117,7 +124,8 @@ def tile_attend_mlp_resid_topk_kernel(tc, qT, k_words, k_scales, c_words, c_scal
             )
         q_grouped = [shared.tile([P, NQ * PACK], BF16, name="q_grouped0", offset=4 * T, align_bytes=64)]
         interleave_q(0, q_grouped[0])
-        c_win = load_words(c_words, "c_win", "A")
+        c_win = load_words(c_words, "c_win", "A0")
+        v_win = [load_v(0)]
 
         q_grouped.append(shared.tile([P, NQ * PACK], BF16, name="q_grouped1", offset=0, align_bytes=64))
         interleave_q(1, q_grouped[1])
@@ -125,7 +133,7 @@ def tile_attend_mlp_resid_topk_kernel(tc, qT, k_words, k_scales, c_words, c_scal
         nb_got = shared.tile([P, N], F32, name="nb_got", offset=4 * T + 4 * N, align_bytes=64)
         nc.vector.tensor_copy(nb_got[:], nb_win[:].indirect(offsets[:]))
 
-        nb_dealt = stream.tile([P, N], F32, name="nb_dealt", offset=4 * T, align_bytes=64)
+        nb_dealt = stream.tile([P, N], F32, name="nb_dealt", offset=STREAM_OFFSETS["B"], align_bytes=64)
         nc.scalar.copy(
             nb_dealt[:].rearrange("p (t g j) -> p t g j", t=PACK, j=4),
             nb_got[:].rearrange("p (g t j) -> p t g j", t=PACK, j=4),
@@ -140,22 +148,16 @@ def tile_attend_mlp_resid_topk_kernel(tc, qT, k_words, k_scales, c_words, c_scal
         us_col = keep.tile([P, PACK], F32, name="us_col")
         nc.scalar.copy(us_col[:], nb_ps[:, 32 : 32 + PACK])
 
-        def load_v(b):
-            win = stream_tile(F32, "v_win%d" % b, "CBA"[b]) if b < 3 else shared.tile([P, T], F32, name="v_win3", offset=0, align_bytes=64)
-            nc.sync.dma_start(out=win[:], in_=vT[b * P : (b + 1) * P, :])
-            return win
-
         kw = gather_words(k_win, shared.tile([P, N], U32, name="kw_got", offset=4 * T, align_bytes=64), "kw")
         q_mx.append(quantize(q_grouped[1][:], NQ, "q1", shared, 4 * T))
-        v_win = [load_v(0), load_v(1)]
+        v_win.extend([load_v(1), load_v(2)])
         cw = gather_words(c_win, shared.tile([P, N], U32, name="cw_got", offset=0, align_bytes=64), "cw")
-        v_win.append(load_v(2))
         v_win.append(load_v(3))
 
         banks = [psum.tile([P, NQ], F32, name="score%d" % t, tag="score%d" % t) for t in range(PACK)]
 
         def score_pass(t, o, words, table, start, stop):
-            col = (t * PASSES + o) * P
+            col = o * N + t * P
             byte = (2 * o + table) * N + t * P
             nc.tensor.matmul_mx(
                 out=banks[t][:],
@@ -177,10 +179,12 @@ def tile_attend_mlp_resid_topk_kernel(tc, qT, k_words, k_scales, c_words, c_scal
             nc.scalar.activation(hidden[:, t * NQ : (t + 1) * NQ], banks[t][:], ACT.Relu, bias=nb_col[:, t : t + 1])
 
         def prepare_v(b):
-            if b < 2:
-                got = keep.tile([P, N], BF16, name="v_got%d" % b, align_bytes=64)
+            if b == 0:
+                got = shared.tile([P, N], BF16, name="v_got0", offset=0, align_bytes=64)
+            elif b == 1:
+                got = keep.tile([P, N], BF16, name="v_got1", align_bytes=64)
             else:
-                got = stream.tile([P, N], BF16, name="v_got%d" % b, offset=4 * T + 2 * N * (b - 2), align_bytes=64)
+                got = stream.tile([P, N], BF16, name="v_got%d" % b, offset=STREAM_OFFSETS["y"] + 2 * N * (b - 2), align_bytes=64)
             nc.vector.tensor_copy(
                 got[:].rearrange("p (u g j w) -> p g u w j", u=2, j=4, w=2),
                 v_win[b][:].indirect(offsets[:]),
@@ -198,15 +202,17 @@ def tile_attend_mlp_resid_topk_kernel(tc, qT, k_words, k_scales, c_words, c_scal
 
         v_grouped = [prepare_v(0), prepare_v(1)]
 
-        y = stream.tile([P, NQ * PACK], BF16, name="y", offset=4 * T, align_bytes=64)
-        nc.vector.tensor_tensor(
+        y_planes = stream.tile([P, PACK * NQ], BF16, name="y_planes", offset=STREAM_OFFSETS["B"], align_bytes=64)
+        for t in range(PACK):
+            cols = slice(t * NQ, (t + 1) * NQ)
+            nc.vector.tensor_scalar(y_planes[:, cols], hidden[:, cols], us_col[:, t : t + 1], None, ALU.mult)
+        y = stream.tile([P, NQ * PACK], BF16, name="y", offset=STREAM_OFFSETS["y"], align_bytes=64)
+        nc.vector.tensor_copy(
             y[:].rearrange("p (c i t) -> p c t i", i=4, t=PACK),
-            hidden[:].rearrange("p (t c i) -> p c t i", i=4, t=PACK),
-            us_col[:].unsqueeze(1).unsqueeze(3).to_broadcast([P, NQ // 4, PACK, 4]),
-            ALU.mult,
+            y_planes[:].rearrange("p (t c i) -> p c t i", i=4, t=PACK),
         )
         y_codes, y_scales = quantize(y[:], NQ, "y")
-        v_mx = [quantize(v_grouped[b][:], P, "v%d" % b, stream, 4 * T + 4 * N + 4 * P * b) for b in range(2)]
+        v_mx = [quantize(v_grouped[b][:], P, "v%d" % b, stream, STREAM_OFFSETS["y"] + 4 * N + 4 * P * b) for b in range(2)]
         v_mx.append(quantize(prepare_v(2)[:], P, "v2"))
 
         out_rows = out[0].rearrange("(a p) e -> p a e", p=P)

@@ -22,7 +22,9 @@ P = 128
 PACK = 4
 PASSES = D // (P * PACK)
 WINDOW = 4 * T
-STREAM_OFFSETS = {"A": WINDOW // 2, "A0": 0, "A1": WINDOW, "B": 2 * WINDOW, "y": 2 * WINDOW + WINDOW // 2, "gap": 3 * WINDOW, "C": 3 * WINDOW + 2 * N}
+HIDDEN_AT = 2 * WINDOW
+Y_AT = 3 * WINDOW
+STREAM_OFFSETS = {"A": WINDOW // 2, "A0": 0, "A1": WINDOW, "B": 2 * WINDOW, "gap": 3 * WINDOW, "C": 3 * WINDOW + 2 * N}
 
 
 def tile_attend_mlp_resid_topk_kernel(tc, qT, k_words, k_scales, c_words, c_scales, vT, nb, us, offs, out):
@@ -96,11 +98,10 @@ def tile_attend_mlp_resid_topk_kernel(tc, qT, k_words, k_scales, c_words, c_scal
         def gather_words(win, got, name):
             nc.vector.tensor_copy(got[:], win[:].indirect(offsets[:]))
             dealt = keep.tile([P, 4 * N], U8, name=name + "_dealt", align_bytes=64)
-            for o in range(PASSES):
-                nc.vector.tensor_copy(
-                    dealt[:].bitcast(U16)[:, o * N : (o + 1) * N].rearrange("p (t g j) -> p t g j", t=PACK, j=4),
-                    got[:].bitcast(U16)[:, o : 2 * N : 2].rearrange("p (g t j) -> p t g j", t=PACK, j=4),
-                )
+            to = dealt[:].bitcast(U16).rearrange("p (t o g j) -> p t g o j", t=PACK, o=PASSES, j=4)
+            words = got[:].bitcast(U16).rearrange("p (g t j o) -> p t g o j", t=PACK, o=PASSES, j=4)
+            for t in range(PACK):
+                nc.vector.tensor_copy(to[:, t], words[:, t])
             return dealt
 
         def quantize(src, width, name, pool=keep, offset=None):
@@ -157,7 +158,7 @@ def tile_attend_mlp_resid_topk_kernel(tc, qT, k_words, k_scales, c_words, c_scal
         banks = [psum.tile([P, NQ], F32, name="score%d" % t, tag="score%d" % t) for t in range(PACK)]
 
         def score_pass(t, o, words, table, start, stop):
-            col = o * N + t * P
+            col = (t * PASSES + o) * P
             byte = (2 * o + table) * N + t * P
             nc.tensor.matmul_mx(
                 out=banks[t][:],
@@ -172,19 +173,15 @@ def tile_attend_mlp_resid_topk_kernel(tc, qT, k_words, k_scales, c_words, c_scal
         for o in range(PASSES):
             for t in range(PACK):
                 score_pass(t, o, kw, 0, o == 0, False)
-        hidden = keep.tile([P, PACK * NQ], F32, name="hidden", tag="hidden", align_bytes=64)
+        hidden = shared.tile([P, PACK * NQ], F32, name="hidden", offset=HIDDEN_AT, align_bytes=64)
         for t in range(PACK):
             for o in range(PASSES):
                 score_pass(t, o, cw, 1, False, o == PASSES - 1)
             nc.scalar.activation(hidden[:, t * NQ : (t + 1) * NQ], banks[t][:], ACT.Relu, bias=nb_col[:, t : t + 1])
 
-        def prepare_v(b):
-            if b == 0:
-                got = shared.tile([P, N], BF16, name="v_got0", offset=0, align_bytes=64)
-            elif b == 1:
-                got = keep.tile([P, N], BF16, name="v_got1", align_bytes=64)
-            else:
-                got = stream.tile([P, N], BF16, name="v_got%d" % b, offset=STREAM_OFFSETS["y"] + 2 * N * (b - 2), align_bytes=64)
+        v_grouped = [keep.tile([P, 2 * P * PACK], BF16, name="v_grouped%d" % h, align_bytes=64) for h in range(2)]
+
+        def prepare_v(b, got):
             nc.vector.tensor_copy(
                 got[:].rearrange("p (u g j w) -> p g u w j", u=2, j=4, w=2),
                 v_win[b][:].indirect(offsets[:]),
@@ -193,54 +190,48 @@ def tile_attend_mlp_resid_topk_kernel(tc, qT, k_words, k_scales, c_words, c_scal
             words = got[:].bitcast(F32)
             for u in range(2):
                 nc.tensor.transpose(turned[:, u * P : (u + 1) * P], words[:, u * P : (u + 1) * P], ident[:])
-            grouped = keep.tile([P, P * PACK], BF16, name="v_grouped%d" % b, align_bytes=64)
             nc.scalar.copy(
-                grouped[:].bitcast(F32).rearrange("p (e u) -> p e u", u=2),
+                v_grouped[b // 2][:].bitcast(F32)[:, (b % 2) * 2 * P : (b % 2 + 1) * 2 * P].rearrange("p (e u) -> p e u", u=2),
                 turned[:].rearrange("p (u e) -> p e u", u=2),
             )
-            return grouped
 
-        v_grouped = [prepare_v(0), prepare_v(1)]
+        prepare_v(0, shared.tile([P, N], BF16, name="v_got0", offset=0, align_bytes=64))
+        prepare_v(1, keep.tile([P, N], BF16, name="v_got1"))
 
         y_planes = stream.tile([P, PACK * NQ], BF16, name="y_planes", offset=STREAM_OFFSETS["B"], align_bytes=64)
         for t in range(PACK):
             cols = slice(t * NQ, (t + 1) * NQ)
             nc.vector.tensor_scalar(y_planes[:, cols], hidden[:, cols], us_col[:, t : t + 1], None, ALU.mult)
-        y = stream.tile([P, NQ * PACK], BF16, name="y", offset=STREAM_OFFSETS["y"], align_bytes=64)
-        nc.vector.tensor_copy(
+        y = shared.tile([P, NQ * PACK], BF16, name="y", offset=Y_AT, align_bytes=64)
+        nc.scalar.copy(
             y[:].rearrange("p (c i t) -> p c t i", i=4, t=PACK),
             y_planes[:].rearrange("p (t c i) -> p c t i", i=4, t=PACK),
         )
-        y_codes, y_scales = quantize(y[:], NQ, "y")
-        v_mx = [quantize(v_grouped[b][:], P, "v%d" % b, stream, STREAM_OFFSETS["y"] + 4 * N + 4 * P * b) for b in range(2)]
-        v_mx.append(quantize(prepare_v(2)[:], P, "v2"))
+        v_mx = [quantize(v_grouped[0][:], 2 * P, "v0", shared, HIDDEN_AT)]
+        for b in (2, 3):
+            prepare_v(b, shared.tile([P, N], BF16, name="v_got%d" % b, offset=HIDDEN_AT + 2 * N * (b - 1), align_bytes=64))
+        y_codes, y_scales = quantize(y[:], NQ, "y", stream, STREAM_OFFSETS["A0"])
+        v_mx.append(quantize(v_grouped[1][:], 2 * P, "v1", shared, Y_AT))
 
         out_rows = out[0].rearrange("(a p) e -> p a e", p=P)
-
-        def finish(b, halves):
-            result = keep.tile([P, PACK * P], F32, name="result%d" % b)
-            for h, (engine, queue) in enumerate(halves):
-                width = PACK // len(halves)
-                acc = psum.tile([P, width * P], F32, name="acc%d_%d" % (b, h), tag="acc%d" % ((b + h + 1) % 2))
-                for i in range(width):
-                    a = h * width + i
+        for h in range(2):
+            for pair in range(2):
+                acc = psum.tile([P, 4 * P], F32, name="acc%d%d" % (h, pair), tag=("turn0", "acc1", "acc2", "acc3")[2 * h + pair])
+                for i in range(2):
+                    rows = slice((2 * pair + i) * P, (2 * pair + i + 1) * P)
                     nc.tensor.matmul_mx(
-                        out=acc[:, i * P : (i + 1) * P],
-                        lhsT=y_codes[:, a * P : (a + 1) * P].bitcast(FP8X4),
-                        lhsT_scale=y_scales[:, a * P : (a + 1) * P],
-                        rhs=v_mx[b][0][:].bitcast(FP8X4),
-                        rhs_scale=v_mx[b][1][:],
+                        out=acc[:, i * 2 * P : (i + 1) * 2 * P],
+                        lhsT=y_codes[:, rows].bitcast(FP8X4),
+                        lhsT_scale=y_scales[:, rows],
+                        rhs=v_mx[h][0][:].bitcast(FP8X4),
+                        rhs_scale=v_mx[h][1][:],
                         start=True,
                         stop=True,
                     )
-                part = result[:, h * width * P : (h + 1) * width * P]
-                engine(part, acc[:])
+                result = keep.tile([P, 4 * P], F32, name="result%d%d" % (h, pair))
+                copy, queue = ((nc.scalar.copy, nc.scalar), (nc.vector.tensor_copy, nc.sync))[pair]
+                copy(result[:], acc[:])
                 queue.dma_start(
-                    out=out_rows[:, h * width : (h + 1) * width, b * P : (b + 1) * P],
-                    in_=part.rearrange("p (a e) -> p a e", e=P),
+                    out=out_rows[:, 2 * pair : 2 * pair + 2, h * 2 * P : (h + 1) * 2 * P],
+                    in_=result[:].rearrange("p (a e) -> p a e", a=2),
                 )
-
-        for b in range(3):
-            finish(b, [(nc.scalar.copy, nc.sync)])
-        v_mx.append(quantize(prepare_v(3)[:], P, "v3"))
-        finish(3, [(nc.scalar.copy, nc.scalar), (nc.vector.tensor_copy, nc.sync)])

from contextlib import ExitStack

import concourse.mybir as mybir
from concourse.masks import make_identity

D, T, N, NQ, DV = 1024, 2048, 512, 512, 512
FLOPS = 2 * (2 * D * N * NQ + N * NQ * DV)
BYTES = 4 * (D * NQ + 2 * 128 * T + DV * T + T + N + NQ * DV) + 2 * 32 * T + 2 * 128 * (N // 16)

F32 = mybir.dt.float32
BF16 = mybir.dt.bfloat16
I32 = mybir.dt.int32
U32 = mybir.dt.uint32
U16 = mybir.dt.uint16
U8 = mybir.dt.uint8
FP8X4 = mybir.dt.float8_e4m3fn_x4
FP4X4 = mybir.dt.float4_e2m1fn_x4
ACT = mybir.ActivationFunctionType
ALU = mybir.AluOpType

P = 128
PACK = 4
PASSES = D // (P * PACK)
WINDOW = 4 * T
HIDDEN_AT = 2 * WINDOW
Y_AT = 3 * WINDOW
STREAM_OFFSETS = {"A": WINDOW // 2, "A0": 0, "A1": WINDOW, "B": 2 * WINDOW, "gap": 3 * WINDOW, "C": 3 * WINDOW + 2 * N}


def tile_attend_mlp_resid_topk_kernel(tc, qT, k_words, k_scales, c_words, c_scales, vT, nb, us, offs, out):
    nc = tc.nc
    with ExitStack() as ctx:
        keep = ctx.enter_context(tc.tile_pool(name="keep", bufs=1))
        shared = ctx.enter_context(tc.tile_pool(name="shared", bufs=1))
        stream = ctx.enter_context(tc.tile_pool(name="stream", bufs=1))
        psum = ctx.enter_context(tc.psum_pool(name="psum", bufs=1))

        offsets = keep.tile([P, N // 16], U16, name="offsets")

        def stream_tile(dtype, name, buffer):
            return stream.tile([P, T], dtype, name=name, offset=STREAM_OFFSETS[buffer], align_bytes=64)

        def load_q(o):
            raw = stream_tile(F32, "q_raw%d" % o, "AB"[o])
            nc.sync.dma_start(out=raw[:], in_=qT[0, 512 * o : 512 * (o + 1), :].rearrange("(p j) w -> p (j w)", j=PACK))
            return raw

        def load_words(words, name, buffer):
            win = stream_tile(U32, name, buffer)
            nc.sync.dma_start(out=win[:].bitcast(I32), in_=words[0].rearrange("p t b -> p (t b)").bitcast(I32))
            return win

        def load_v(b):
            win = stream_tile(F32, "v_win%d" % b, ("A1", "B", "C", "A0")[b])
            nc.sync.dma_start(out=win[:], in_=vT[b * P : (b + 1) * P, :])
            return win

        def load_scales(scales, win):
            nc.vector.memset(win[:].bitcast(I32), 0)
            nc.sync.dma_start(out=win[0:P:4, :].bitcast(I32), in_=scales.bitcast(I32).rearrange("o f t -> f o t"))

        nc.sync.dma_start(offsets[:], offs)
        q_raw = [load_q(0)]

        ks_win = keep.tile([P, T], U8, name="ks_win")
        load_scales(k_scales, ks_win)
        cs_win = keep.tile([P, T], U8, name="cs_win")
        load_scales(c_scales, cs_win)
        nb_win = keep.tile([P, T], F32, name="nb_win")
        nc.vector.memset(nb_win[:], 0.0)
        nc.sync.dma_start(out=nb_win[0:1, :], in_=nb[0:1, :])

        zeros = stream.tile([P, 3 * P], F32, name="zeros", offset=STREAM_OFFSETS["gap"] - 2 * P, align_bytes=64)
        nc.vector.memset(zeros[:, 0:P], 0.0)
        us_rows = keep.tile([P, P], F32, name="us_rows")
        nc.scalar.activation(us_rows[:], zeros[:, 0:P], ACT.Relu)
        q_raw.append(load_q(1))
        k_win = load_words(k_words, "k_win", "C")
        nc.scalar.dma_start(
            out=us_rows[32 : 32 + PACK, :].rearrange("t (g j) -> t g j", j=4),
            in_=us[0].rearrange("(g t j) one -> t g (j one)", t=PACK, j=4),
        )
        ident = keep.tile([P, P], F32, name="ident")
        make_identity(nc, ident[:])

        scales_dealt = stream.tile([P, 2 * N], U8, name="scales_dealt", offset=STREAM_OFFSETS["gap"], align_bytes=64)
        planes = keep.tile([P, PASSES * 2 * N], U8, name="planes", align_bytes=64)
        nc.vector.memset(planes[:].bitcast(I32), 0)

        def gather_scales(win, table):
            got = keep.tile([P, N], U8, name="scales_got%d" % table)
            nc.vector.tensor_copy(got[:], win[:].indirect(offsets[:]))
            nc.vector.tensor_copy(
                scales_dealt[:, table * N : (table + 1) * N].bitcast(I32).rearrange("p (t g) -> p t g", t=PACK),
                got[:].bitcast(I32).rearrange("p (g t) -> p t g", t=PACK),
            )

        def gather_words(win, got, name):
            nc.vector.tensor_copy(got[:], win[:].indirect(offsets[:]))
            dealt = keep.tile([P, 4 * N], U8, name=name + "_dealt", align_bytes=64)
            to = dealt[:].bitcast(U16).rearrange("p (t o g j) -> p t g o j", t=PACK, o=PASSES, j=4)
            words = got[:].bitcast(U16).rearrange("p (g t j o) -> p t g o j", t=PACK, o=PASSES, j=4)
            for t in range(PACK):
                nc.vector.tensor_copy(to[:, t], words[:, t])
            return dealt

        def quantize(src, width, name, pool=keep, offset=None):
            codes = pool.tile([P, width], U32, name=name + "_codes", offset=offset, align_bytes=64)
            scales = keep.tile([P, width], U8, name=name + "_scales", align_bytes=64)
            nc.vector.quantize_mx(out=codes[:].bitcast(FP8X4), scales=scales[:], in_=src)
            return codes, scales

        def interleave_q(o, grouped):
            nc.scalar.copy(
                grouped[:].rearrange("p (c i t) -> p c t i", i=4, t=PACK),
                q_raw[o][:].rearrange("p (t c i) -> p c t i", i=4, t=PACK),
            )

        gather_scales(ks_win, 0)
        gather_scales(cs_win, 1)
        for quad in range(4):
            nc.sync.dma_start(
                out=planes[32 * quad : 32 * quad + 4, :].bitcast(I32).rearrange("i (o w) -> i o w", o=PASSES),
                in_=scales_dealt[32 * quad : 32 * (quad + 1) : 4, :].bitcast(I32),
            )
        q_grouped = [shared.tile([P, NQ * PACK], BF16, name="q_grouped0", offset=4 * T, align_bytes=64)]
        interleave_q(0, q_grouped[0])
        c_win = load_words(c_words, "c_win", "A0")
        v_win = [load_v(0)]

        q_grouped.append(shared.tile([P, NQ * PACK], BF16, name="q_grouped1", offset=0, align_bytes=64))
        interleave_q(1, q_grouped[1])
        q_mx = [quantize(q_grouped[0][:], NQ, "q0")]
        nb_got = shared.tile([P, N], F32, name="nb_got", offset=4 * T + 4 * N, align_bytes=64)
        nc.vector.tensor_copy(nb_got[:], nb_win[:].indirect(offsets[:]))

        nb_dealt = stream.tile([P, N], F32, name="nb_dealt", offset=STREAM_OFFSETS["B"], align_bytes=64)
        nc.scalar.copy(
            nb_dealt[:].rearrange("p (t g j) -> p t g j", t=PACK, j=4),
            nb_got[:].rearrange("p (g t j) -> p t g j", t=PACK, j=4),
        )
        nb_ps = psum.tile([P, N], F32, name="nb_ps", tag="turn0")
        nc.tensor.matmul(nb_ps[:, 0:P], us_rows[:], ident[:], start=True, stop=False, is_transpose=True)
        nc.tensor.matmul(nb_ps[:, 0:P], nb_dealt[:, 0:P], ident[:], start=False, stop=True, is_transpose=True)
        for t in range(1, PACK):
            nc.tensor.transpose(nb_ps[:, t * P : (t + 1) * P], nb_dealt[:, t * P : (t + 1) * P], ident[:])
        nb_col = keep.tile([P, PACK], F32, name="nb_col")
        nc.scalar.copy(nb_col[:], nb_ps[:, 0:N:P])
        us_col = keep.tile([P, PACK], F32, name="us_col")
        nc.scalar.copy(us_col[:], nb_ps[:, 32 : 32 + PACK])

        kw = gather_words(k_win, shared.tile([P, N], U32, name="kw_got", offset=4 * T, align_bytes=64), "kw")
        q_mx.append(quantize(q_grouped[1][:], NQ, "q1", shared, 4 * T))
        v_win.extend([load_v(1), load_v(2)])
        cw = gather_words(c_win, shared.tile([P, N], U32, name="cw_got", offset=0, align_bytes=64), "cw")
        v_win.append(load_v(3))

        banks = [psum.tile([P, NQ], F32, name="score%d" % t, tag="score%d" % t) for t in range(PACK)]

        def score_pass(t, o, words, table, start, stop):
            col = (t * PASSES + o) * P
            byte = (2 * o + table) * N + t * P
            nc.tensor.matmul_mx(
                out=banks[t][:],
                lhsT=words[:, 2 * col : 2 * (col + P)].bitcast(FP4X4),
                lhsT_scale=planes[:, byte : byte + P],
                rhs=q_mx[o][0][:].bitcast(FP8X4),
                rhs_scale=q_mx[o][1][:],
                start=start,
                stop=stop,
            )

        for o in range(PASSES):
            for t in range(PACK):
                score_pass(t, o, kw, 0, o == 0, False)
        hidden = shared.tile([P, PACK * NQ], F32, name="hidden", offset=HIDDEN_AT, align_bytes=64)
        for t in range(PACK):
            for o in range(PASSES):
                score_pass(t, o, cw, 1, False, o == PASSES - 1)
            nc.scalar.activation(hidden[:, t * NQ : (t + 1) * NQ], banks[t][:], ACT.Relu, bias=nb_col[:, t : t + 1])

        v_grouped = [keep.tile([P, 2 * P * PACK], BF16, name="v_grouped%d" % h, align_bytes=64) for h in range(2)]

        def prepare_v(b, got):
            nc.vector.tensor_copy(
                got[:].rearrange("p (u g j w) -> p g u w j", u=2, j=4, w=2),
                v_win[b][:].indirect(offsets[:]),
            )
            turned = psum.tile([P, 2 * P], F32, name="turned%d" % b, tag="score%d" % (1, 3, 0, 2)[b])
            words = got[:].bitcast(F32)
            for u in range(2):
                nc.tensor.transpose(turned[:, u * P : (u + 1) * P], words[:, u * P : (u + 1) * P], ident[:])
            nc.scalar.copy(
                v_grouped[b // 2][:].bitcast(F32)[:, (b % 2) * 2 * P : (b % 2 + 1) * 2 * P].rearrange("p (e u) -> p e u", u=2),
                turned[:].rearrange("p (u e) -> p e u", u=2),
            )

        prepare_v(0, shared.tile([P, N], BF16, name="v_got0", offset=0, align_bytes=64))
        prepare_v(1, keep.tile([P, N], BF16, name="v_got1"))

        y_planes = stream.tile([P, PACK * NQ], BF16, name="y_planes", offset=STREAM_OFFSETS["B"], align_bytes=64)
        for t in range(PACK):
            cols = slice(t * NQ, (t + 1) * NQ)
            nc.vector.tensor_scalar(y_planes[:, cols], hidden[:, cols], us_col[:, t : t + 1], None, ALU.mult)
        y = shared.tile([P, NQ * PACK], BF16, name="y", offset=Y_AT, align_bytes=64)
        nc.scalar.copy(
            y[:].rearrange("p (c i t) -> p c t i", i=4, t=PACK),
            y_planes[:].rearrange("p (t c i) -> p c t i", i=4, t=PACK),
        )
        v_mx = [quantize(v_grouped[0][:], 2 * P, "v0", shared, HIDDEN_AT)]
        for b in (2, 3):
            prepare_v(b, shared.tile([P, N], BF16, name="v_got%d" % b, offset=HIDDEN_AT + 2 * N * (b - 1), align_bytes=64))
        y_codes, y_scales = quantize(y[:], NQ, "y", stream, STREAM_OFFSETS["A0"])
        v_mx.append(quantize(v_grouped[1][:], 2 * P, "v1", shared, Y_AT))

        out_rows = out[0].rearrange("(a p) e -> p a e", p=P)
        for h in range(2):
            for pair in range(2):
                acc = psum.tile([P, 4 * P], F32, name="acc%d%d" % (h, pair), tag=("turn0", "acc1", "acc2", "acc3")[2 * h + pair])
                for i in range(2):
                    rows = slice((2 * pair + i) * P, (2 * pair + i + 1) * P)
                    nc.tensor.matmul_mx(
                        out=acc[:, i * 2 * P : (i + 1) * 2 * P],
                        lhsT=y_codes[:, rows].bitcast(FP8X4),
                        lhsT_scale=y_scales[:, rows],
                        rhs=v_mx[h][0][:].bitcast(FP8X4),
                        rhs_scale=v_mx[h][1][:],
                        start=True,
                        stop=True,
                    )
                result = keep.tile([P, 4 * P], F32, name="result%d%d" % (h, pair))
                copy, queue = ((nc.scalar.copy, nc.scalar), (nc.vector.tensor_copy, nc.sync))[pair]
                copy(result[:], acc[:])
                queue.dma_start(
                    out=out_rows[:, 2 * pair : 2 * pair + 2, h * 2 * P : (h + 1) * 2 * P],
                    in_=result[:].rearrange("p (a e) -> p a e", a=2),
                )
